import numpy as np
import ml_dtypes

BF16 = ml_dtypes.bfloat16


def bf(x):
    return np.asarray(x, np.float32).astype(BF16)


def f32(x):
    return np.asarray(x, np.float32)


def f64(x):
    return np.asarray(x).astype(np.float64)


def striped(idx):
    return np.tile(idx.reshape(-1, 16).T, (8, 1))


S, K, M, N, E, Q, O = 256, 256, 256, 192, 1, 192, 256


def sigmoid(v):
    return 1.0 / (1.0 + np.exp(-v))


def setup_inputs():
    return {"base": bf(np.random.standard_normal((M, S))), "x": bf(np.random.standard_normal((K, N))), "w": bf(1.2 * np.random.standard_normal((E, K, M)) / np.sqrt(K)), "w2": bf(np.random.standard_normal((M, O)) / np.sqrt(2 * M)), "b": f32(0.5 * np.random.standard_normal((O, 1))), "offs": striped(np.random.permutation(S)[:N])}


def reference(base, x, w, w2, b, offs):
    idx = offs[:16].T.reshape(-1)
    z = f64(base).copy()
    for e in range(E):
        z[:, idx[e * Q : (e + 1) * Q]] += f64(w)[e].T @ f64(x)[:, e * Q : (e + 1) * Q]
    y = f64(w2).T @ z
    return (y + f64(b)) * sigmoid(y + f64(b))

@@ -1,0 +1,71 @@
+import concourse.mybir as mybir
+from concourse.masks import make_identity
+
+P = 128
+S, K, M, N, O = 256, 256, 256, 192, 256
+KB, MB, OB = K // P, M // P, O // P
+FLOPS = 2 * K * M * N + 2 * M * O * S
+BF16, F32, U16 = mybir.dt.bfloat16, mybir.dt.float32, mybir.dt.uint16
+
+
+def tile_rows_thenproj_silu_kernel(tc, base, x, w, w2, b, offs, out):
+    nc = tc.nc
+    silu = mybir.ActivationFunctionType.Silu
+    with (
+        tc.tile_pool(name="held", bufs=1) as held,
+        tc.psum_pool(name="psum", bufs=1) as psum,
+    ):
+        base_tile = held.tile([P, MB, S], BF16)
+        x_tile = held.tile([P, KB, N], BF16)
+        w_tile = held.tile([P, KB, M], BF16)
+        w2_tile = held.tile([P, MB, O], BF16)
+        bias = held.tile([P, OB], F32)
+        offsets = held.tile([P, N // 16], U16)
+
+        nc.sync.dma_start(base_tile[:], base.rearrange("(a p) s -> p a s", p=P))
+        nc.sync.dma_start(w_tile[:], w.rearrange("e (a p) m -> p (e a) m", p=P))
+        nc.sync.dma_start(x_tile[:], x.rearrange("(a p) n -> p a n", p=P))
+        nc.sync.dma_start(offsets[:], offs)
+        nc.sync.dma_start(w2_tile[:], w2.rearrange("(a p) o -> p a o", p=P))
+        nc.sync.dma_start(bias[:], b.rearrange("(a p) o -> p (a o)", p=P))
+
+        ident = held.tile([P, P], BF16)
+        make_identity(nc, ident[:])
+
+        windows = []
+        for mb in range(MB):
+            window = psum.tile([P, S], F32, name=f"window{mb}")
+            nc.tensor.matmul(window[:], ident[:], base_tile[:, mb, :], start=True, stop=False)
+            windows.append(window)
+
+        for mb in range(MB):
+            for kb in range(KB):
+                nc.tensor.matmul(
+                    windows[mb][:].indirect(offsets[:]),
+                    w_tile[:, kb, mb * P : (mb + 1) * P],
+                    x_tile[:, kb, :],
+                    start=False,
+                    stop=kb == KB - 1,
+                )
+
+        z = []
+        for mb in range(MB):
+            z_block = held.tile([P, S], BF16, name=f"z{mb}")
+            nc.vector.tensor_copy(z_block[:], windows[mb][:])
+            z.append(z_block)
+
+        y = [psum.tile([P, S], F32, name=f"y{ob}") for ob in range(OB)]
+        for mb in range(MB):
+            for ob in range(OB):
+                nc.tensor.matmul(
+                    y[ob][:],
+                    w2_tile[:, mb, ob * P : (ob + 1) * P],
+                    z[mb][:],
+                    start=mb == 0,
+                    stop=mb == MB - 1,
+                )
+
+        for ob in range(OB):
+            out_block = held.tile([P, S], F32, name=f"out{ob}")
+            nc.scalar.activation(out_block[:], y[ob][:], silu, bias=bias[:, ob : ob + 1])
+            nc.sync.dma_start(out[ob * P : (ob + 1) * P, :], out_block[:])

@@ -4,6 +4,8 @@ from concourse.masks import make_identity
 P = 128
 S, K, M, N, O = 256, 256, 256, 192, 256
 KB, MB, OB = K // P, M // P, O // P
+WARM_COLUMNS = 512
+WARM_MATMULS = 4
 FLOPS = 2 * K * M * N + 2 * M * O * S
 BF16, F32, U16 = mybir.dt.bfloat16, mybir.dt.float32, mybir.dt.uint16
 
@@ -31,6 +33,14 @@ def tile_rows_thenproj_silu_kernel(tc, base, x, w, w2, b, offs, out):
 
         ident = held.tile([P, P], BF16)
         make_identity(nc, ident[:])
+
+        zeros = held.tile([P, WARM_COLUMNS], BF16)
+        nc.vector.memset(zeros[:], 0.0)
+        spare = psum.tile([P, WARM_COLUMNS], F32)
+        for i in range(WARM_MATMULS):
+            nc.tensor.matmul(spare[:], zeros[:, :P], zeros[:], start=True, stop=True)
+        first_silu = held.tile([P, 1], F32)
+        nc.scalar.activation(first_silu[:], zeros[:, :1], silu)
 
         windows = []
         for mb in range(MB):

@@ -4,8 +4,10 @@ from concourse.masks import make_identity
 P = 128
 S, K, M, N, O = 256, 256, 256, 192, 256
 KB, MB, OB = K // P, M // P, O // P
-WARM_COLUMNS = 512
-WARM_MATMULS = 4
+WARM_COLUMNS = 256
+WARM_MATMULS = 5
+HALVES = 2
+H = S // HALVES
 FLOPS = 2 * K * M * N + 2 * M * O * S
 BF16, F32, U16 = mybir.dt.bfloat16, mybir.dt.float32, mybir.dt.uint16
 
@@ -25,8 +27,8 @@ def tile_rows_thenproj_silu_kernel(tc, base, x, w, w2, b, offs, out):
         offsets = held.tile([P, N // 16], U16)
 
         nc.sync.dma_start(base_tile[:], base.rearrange("(a p) s -> p a s", p=P))
-        nc.sync.dma_start(w_tile[:], w.rearrange("e (a p) m -> p (e a) m", p=P))
-        nc.sync.dma_start(x_tile[:], x.rearrange("(a p) n -> p a n", p=P))
+        nc.sync.dma_start(w_tile[:], w.rearrange("e (p a) m -> p (e a) m", p=P))
+        nc.sync.dma_start(x_tile[:], x.rearrange("(p a) n -> p a n", p=P))
         nc.sync.dma_start(offsets[:], offs)
         nc.sync.dma_start(w2_tile[:], w2.rearrange("(a p) o -> p a o", p=P))
         nc.sync.dma_start(bias[:], b.rearrange("(a p) o -> p (a o)", p=P))
@@ -61,21 +63,26 @@ def tile_rows_thenproj_silu_kernel(tc, base, x, w, w2, b, offs, out):
         z = []
         for mb in range(MB):
             z_block = held.tile([P, S], BF16, name=f"z{mb}")
-            nc.vector.tensor_copy(z_block[:], windows[mb][:])
+            for h in range(HALVES):
+                cols = slice(h * H, (h + 1) * H)
+                nc.vector.tensor_copy(z_block[:, cols], windows[mb][:, cols])
             z.append(z_block)
 
-        y = [psum.tile([P, S], F32, name=f"y{ob}") for ob in range(OB)]
+        y = [[psum.tile([P, H], F32, name=f"y{h}{ob}") for ob in range(OB)] for h in range(HALVES)]
         for mb in range(MB):
-            for ob in range(OB):
-                nc.tensor.matmul(
-                    y[ob][:],
-                    w2_tile[:, mb, ob * P : (ob + 1) * P],
-                    z[mb][:],
-                    start=mb == 0,
-                    stop=mb == MB - 1,
-                )
+            for h in range(HALVES):
+                for ob in range(OB):
+                    nc.tensor.matmul(
+                        y[h][ob][:],
+                        w2_tile[:, mb, ob * P : (ob + 1) * P],
+                        z[mb][:, h * H : (h + 1) * H],
+                        start=mb == 0,
+                        stop=mb == MB - 1,
+                    )
 
-        for ob in range(OB):
-            out_block = held.tile([P, S], F32, name=f"out{ob}")
-            nc.scalar.activation(out_block[:], y[ob][:], silu, bias=bias[:, ob : ob + 1])
-            nc.sync.dma_start(out[ob * P : (ob + 1) * P, :], out_block[:])
+        out_by_block = out.rearrange("(a p) s -> p a s", p=P)
+        for h in range(HALVES):
+            out_half = held.tile([P, OB, H], F32, name=f"out{h}")
+            for ob in range(OB):
+                nc.scalar.activation(out_half[:, ob, :], y[h][ob][:], silu, bias=bias[:, ob : ob + 1])
+            nc.sync.dma_start(out_by_block[:, :, h * H : (h + 1) * H], out_half[:])

import concourse.mybir as mybir
from concourse.masks import make_identity

P = 128
S, K, M, N, O = 256, 256, 256, 192, 256
KB, MB, OB = K // P, M // P, O // P
WARM_COLUMNS = 256
WARM_MATMULS = 5
HALVES = 2
H = S // HALVES
FLOPS = 2 * K * M * N + 2 * M * O * S
BF16, F32, U16 = mybir.dt.bfloat16, mybir.dt.float32, mybir.dt.uint16


def tile_rows_thenproj_silu_kernel(tc, base, x, w, w2, b, offs, out):
    nc = tc.nc
    silu = mybir.ActivationFunctionType.Silu
    with (
        tc.tile_pool(name="held", bufs=1) as held,
        tc.psum_pool(name="psum", bufs=1) as psum,
    ):
        base_tile = held.tile([P, MB, S], BF16)
        x_tile = held.tile([P, KB, N], BF16)
        w_tile = held.tile([P, KB, M], BF16)
        w2_tile = held.tile([P, MB, O], BF16)
        bias = held.tile([P, OB], F32)
        offsets = held.tile([P, N // 16], U16)

        nc.sync.dma_start(base_tile[:], base.rearrange("(a p) s -> p a s", p=P))
        nc.sync.dma_start(w_tile[:], w.rearrange("e (p a) m -> p (e a) m", p=P))
        nc.sync.dma_start(x_tile[:], x.rearrange("(p a) n -> p a n", p=P))
        nc.sync.dma_start(offsets[:], offs)
        nc.sync.dma_start(w2_tile[:], w2.rearrange("(a p) o -> p a o", p=P))
        nc.sync.dma_start(bias[:], b.rearrange("(a p) o -> p (a o)", p=P))

        ident = held.tile([P, P], BF16)
        make_identity(nc, ident[:])

        zeros = held.tile([P, WARM_COLUMNS], BF16)
        nc.vector.memset(zeros[:], 0.0)
        spare = psum.tile([P, WARM_COLUMNS], F32)
        for i in range(WARM_MATMULS):
            nc.tensor.matmul(spare[:], zeros[:, :P], zeros[:], start=True, stop=True)
        first_silu = held.tile([P, 1], F32)
        nc.scalar.activation(first_silu[:], zeros[:, :1], silu)

        windows = []
        for mb in range(MB):
            window = psum.tile([P, S], F32, name=f"window{mb}")
            nc.tensor.matmul(window[:], ident[:], base_tile[:, mb, :], start=True, stop=False)
            windows.append(window)

        for mb in range(MB):
            for kb in range(KB):
                nc.tensor.matmul(
                    windows[mb][:].indirect(offsets[:]),
                    w_tile[:, kb, mb * P : (mb + 1) * P],
                    x_tile[:, kb, :],
                    start=False,
                    stop=kb == KB - 1,
                )

        z = []
        for mb in range(MB):
            z_block = held.tile([P, S], BF16, name=f"z{mb}")
            for h in range(HALVES):
                cols = slice(h * H, (h + 1) * H)
                nc.vector.tensor_copy(z_block[:, cols], windows[mb][:, cols])
            z.append(z_block)

        y = [[psum.tile([P, H], F32, name=f"y{h}{ob}") for ob in range(OB)] for h in range(HALVES)]
        for mb in range(MB):
            for h in range(HALVES):
                for ob in range(OB):
                    nc.tensor.matmul(
                        y[h][ob][:],
                        w2_tile[:, mb, ob * P : (ob + 1) * P],
                        z[mb][:, h * H : (h + 1) * H],
                        start=mb == 0,
                        stop=mb == MB - 1,
                    )

        out_by_block = out.rearrange("(a p) s -> p a s", p=P)
        for h in range(HALVES):
            out_half = held.tile([P, OB, H], F32, name=f"out{h}")
            for ob in range(OB):
                nc.scalar.activation(out_half[:, ob, :], y[h][ob][:], silu, bias=bias[:, ob : ob + 1])
            nc.sync.dma_start(out_by_block[:, :, h * H : (h + 1) * H], out_half[:])
